import numpy as np
import ml_dtypes


def mxq(x, axis, fmt="e4m3"):
    dtype, down = {"e4m3": (ml_dtypes.float8_e4m3fn, 7), "e5m2": (ml_dtypes.float8_e5m2, 14)}[fmt]
    v = np.moveaxis(np.asarray(x, np.float32).astype(ml_dtypes.bfloat16).astype(np.float64), axis, -1)
    blocks = v.reshape(v.shape[:-1] + (-1, 32))
    amax = np.abs(blocks).max(-1, keepdims=True)
    byte = np.maximum(np.where(amax > 0, np.frexp(amax)[1] - 1 + 127, 0) - down, 1)
    scale = np.exp2(byte - 127.0)
    codes = (blocks / scale).astype(np.float32).astype(dtype).astype(np.float64)
    return np.moveaxis((codes * scale).reshape(v.shape), -1, axis)


WIDE = False


def mx_kscale(k):
    if not WIDE:
        return np.ones(k)
    levels = np.array([10, -10, 5, -5, 0])
    if k % 512:
        return np.exp2(np.random.permutation(np.resize(levels, k // 32))).repeat(32)
    a = np.empty((k // 512, 16))
    for p in range(k // 512):
        a[p, :8] = np.random.permutation(np.resize(levels, 8))
        for g in range(8):
            far = levels[np.abs(levels - a[p, g]) >= 10]
            a[p, g + 8] = far[np.random.randint(len(far))]
    return np.exp2(a.ravel()).repeat(32)


def f64(x):
    return np.asarray(x).astype(np.float64)


def striped(idx):
    return np.tile(np.asarray(idx).reshape(-1, 16).T, (8, 1)).astype(np.uint16)


def unstriped(offs):
    return offs[:16].T.reshape(-1).astype(np.int64)


E2M1 = np.array([0.0, 0.5, 1.0, 1.5, 2.0, 3.0, 4.0, 6.0, -0.0, -0.5, -1.0, -1.5, -2.0, -3.0, -4.0, -6.0])


def pack_weight(w, fmt):
    k, n = w.shape
    w = f64(np.asarray(w, np.float32).astype(ml_dtypes.bfloat16)).reshape(k // 32, 32, n)
    amax = np.abs(w).max(1)
    if fmt == "e4m3":
        byte = np.frexp(amax)[1] - 1 + 127 - 7
    else:
        mant, ex = np.frexp(amax / 6.0)
        byte = np.where(mant > 0.5, ex, ex - 1) + 127
    byte = np.clip(np.where(amax > 0, byte, 1), 1, 254)
    scaled = (w * np.exp2(127.0 - byte)[:, None, :]).reshape(k, n).astype(np.float32)
    by_word = np.ascontiguousarray(scaled.reshape(k // 512, 128, 4, n).transpose(0, 1, 3, 2))
    if fmt == "e4m3":
        words = by_word.astype(ml_dtypes.float8_e4m3fn).view(np.uint8)
    else:
        c = by_word.astype(ml_dtypes.float4_e2m1fn).view(np.uint8) & 0xF
        words = (c[..., 0::2] | (c[..., 1::2] << 4)).reshape(k // 512, 128, 2 * n)
    return np.ascontiguousarray(words), np.ascontiguousarray(byte.astype(np.uint8).reshape(k // 512, 16, n))


def unpack_weight(words, scales, fmt):
    g, _, n = scales.shape
    words = np.ascontiguousarray(words).reshape(g, 128, n, -1)
    if fmt == "e4m3":
        vals = words.view(ml_dtypes.float8_e4m3fn).astype(np.float64)
    else:
        nib = np.empty((g, 128, n, 4), np.uint8)
        nib[..., 0::2] = words & 0xF
        nib[..., 1::2] = words >> 4
        vals = E2M1[nib]
    vals = vals * np.repeat(np.exp2(scales.astype(np.float64) - 127.0), 8, axis=1)[..., None]
    return vals.transpose(0, 1, 3, 2).reshape(g * 512, n)


def sigmoid(v):
    return 1.0 / (1.0 + np.exp(-v))


D, E, T, I, Q = 512, 512, 2048, 512, 128


def setup_inputs():
    n = np.random.standard_normal
    idx = np.random.permutation(T)[:I]
    fd = mx_kscale(D)
    fe = mx_kscale(E)
    keysp = pack_weight(n((D, T)) / fd[:, None], "e4m3")
    valsp = pack_weight(n((E, T)) / fe[:, None], "e4m3")
    return {
        "query": (n((D, Q)) * 0.8 / np.sqrt(D) * fd[:, None]).astype(np.float32),
        "keys_words": keysp[0],
        "keys_scales": keysp[1],
        "th": (np.random.uniform(0.4, 1.0, (Q, 1))).astype(np.float32),
        "gout": (n((E, Q)) * 1 / np.sqrt(E) * fe[:, None]).astype(np.float32),
        "vals_words": valsp[0],
        "vals_scales": valsp[1],
        "dquery": (n((D, Q)) * 1.0 / np.sqrt(D) * fd[:, None]).astype(np.float32),
        "base": (0.5 * n((Q, T))).astype(np.float32),
        "offs": striped(idx),
    }


def reference(query, keys_words, keys_scales, th, gout, vals_words, vals_scales, dquery, base, offs):
    idx = unstriped(offs)
    keysu = unpack_weight(keys_words, keys_scales, "e4m3")
    valsu = unpack_weight(vals_words, vals_scales, "e4m3")
    queryq = mxq(f64(query), 0, "e4m3")
    keysidxg = keysu[:, idx]
    a = queryq.T @ keysidxg
    dqueryq = mxq(f64(dquery), 0, "e4m3")
    ta = dqueryq.T @ keysidxg
    e1s = sigmoid((f64(th) - np.mean(np.square(a), axis=1, keepdims=True)) * 4.0)
    p = np.exp(a - np.max(a, axis=1, keepdims=True))
    z = np.sum(p, axis=1, keepdims=True)
    goutq = mxq(f64(gout), 0, "e4m3")
    valsidxg = valsu[:, idx]
    c0 = goutq.T @ valsidxg
    dz = np.sum(c0 * (1.0 - e1s) * p / np.square(z) * (-1.0), axis=1, keepdims=True)
    dp = c0 * (1.0 - e1s) / z + dz
    de1s = np.sum(c0, axis=1, keepdims=True) / 512.0 - np.sum(c0 * p / z, axis=1, keepdims=True)
    te1s = np.mean(ta * a * 2.0, axis=1, keepdims=True) * (-1.0) * 4.0 * e1s * (1.0 - e1s)
    tp = ta * p
    tz = np.sum(tp, axis=1, keepdims=True)
    tdz = np.sum((te1s * (-1.0) * c0 * p + tp * c0 * (1.0 - e1s) - tz * z * 2.0 * c0 * (1.0 - e1s) * p / np.square(z)) / np.square(z) * (-1.0), axis=1, keepdims=True)
    tdp = (te1s * (-1.0) * c0 - tz * c0 * (1.0 - e1s) / z) / z + tdz
    tde1s = np.sum((tp - tz * p / z) / z * c0, axis=1, keepdims=True) * (-1.0)
    tda = tdp * p + tp * dp + (((tde1s * e1s + te1s * de1s) * (1.0 - e1s) + te1s * (-1.0) * de1s * e1s) * 4.0 * (-1.0) / 512.0 * a + ta * de1s * e1s * (1.0 - e1s) * 4.0 * (-1.0) / 512.0) * 2.0
    gs = tda * 512.0
    gf = np.zeros((Q, T))
    gf[:, idx] = gs
    y = f64(base) + gf
    return y

@@ -1,0 +1,172 @@
+from contextlib import ExitStack
+
+import concourse.mybir as mybir
+
+F32 = mybir.dt.float32
+BF16 = mybir.dt.bfloat16
+I32 = mybir.dt.int32
+U32 = mybir.dt.uint32
+U16 = mybir.dt.uint16
+U8 = mybir.dt.uint8
+FP8X4 = mybir.dt.float8_e4m3fn_x4
+ALU = mybir.AluOpType
+ACT = mybir.ActivationFunctionType
+
+P = 128
+PACK = 4
+TOKENS = 2048
+SLOTS = 512
+ROWS = 128
+FEATURES = 512
+VALS_PLANE = 4
+OUT_CHUNK = 512
+
+FLOPS = 3 * 2 * FEATURES * ROWS * SLOTS
+
+
+def tile_attend_hvevenbyspread_s_kernel(tc, query, keys_words, keys_scales, th, gout, vals_words, vals_scales,
+                                         dquery, base, offs, out):
+    nc = tc.nc
+    with ExitStack() as ctx:
+        sb = ctx.enter_context(tc.tile_pool(name="sb", bufs=1))
+        ps = ctx.enter_context(tc.psum_pool(name="ps", bufs=1))
+
+        def col(name):
+            return sb.tile([P, 1], F32, name=name)
+
+        def wide(name):
+            return sb.tile([P, SLOTS], F32, name=name)
+
+        def words_view(words):
+            return words[0].rearrange("p n t -> p (n t)").bitcast(I32)
+
+        def load_scale_rows(queue, window, scales, first):
+            for quad in range(4):
+                row = 32 * quad + first
+                queue.dma_start(out=window[row:row + 4, :].bitcast(I32),
+                                in_=scales[0, 4 * quad:4 * quad + 4, :].bitcast(I32))
+
+        def interleave(name, raw):
+            grouped = sb.tile([P, ROWS * PACK], BF16, name=name + "_bf16", tag=name + "_bf16", align_bytes=64)
+            nc.scalar.activation(out=grouped[:].rearrange("p (c i t) -> p c t i", i=4, t=PACK),
+                                 in_=raw[:].rearrange("p t (c i) -> p c t i", i=4), func=ACT.Copy)
+            return grouped
+
+        def quantise(name, grouped):
+            codes = sb.tile([P, ROWS], U32, name=name + "_codes", align_bytes=64)
+            plane = sb.tile([P, ROWS], U8, name=name + "_plane", align_bytes=64)
+            nc.vector.quantize_mx(out=codes[:].bitcast(FP8X4), scales=plane[:], in_=grouped[:])
+            return codes, plane
+
+        def product(name, rows_q, words, plane):
+            acc = ps.tile([ROWS, SLOTS], F32, name=name)
+            nc.tensor.matmul_mx(out=acc[:], lhsT=rows_q[0][:].bitcast(FP8X4), lhsT_scale=rows_q[1][:],
+                                rhs=words[:].bitcast(FP8X4), rhs_scale=plane, start=True, stop=True)
+            return acc
+
+        def affine(name, x, scale, bias=0.0):
+            y = col(name)
+            nc.scalar.activation(out=y[:], in_=x[:], func=ACT.Identity, scale=scale, bias=bias)
+            return y
+
+        offsets = sb.tile([P, SLOTS // 16], U16, name="offsets")
+        nc.sync.dma_start(offsets[:], offs)
+        key_scale_pool = sb.tile([P, TOKENS], U8, name="key_scale_pool", tag="key_scales_then_value_words")
+        val_scale_pool = sb.tile([P, TOKENS], U8, name="val_scale_pool")
+        nc.vector.memset(key_scale_pool[:].bitcast(I32), 0)
+        nc.vector.memset(val_scale_pool[:].bitcast(I32), 0)
+        placed = sb.tile([P, TOKENS], F32, name="placed")
+        nc.vector.memset(placed[:], 0.0)
+
+        key_word_pool = sb.tile([P, TOKENS], U32, name="key_word_pool", tag="key_words_then_base")
+        nc.sync.dma_start(out=key_word_pool[:].bitcast(I32), in_=words_view(keys_words))
+        load_scale_rows(nc.scalar, key_scale_pool, keys_scales, 0)
+        q_raw = sb.tile([P, PACK, ROWS], F32, name="q_raw", tag="query_then_gout")
+        nc.sync.dma_start(out=q_raw[:], in_=query.rearrange("(p t) q -> p t q", t=PACK))
+        dq_raw = sb.tile([P, PACK, ROWS], F32, name="dq_raw")
+        nc.sync.dma_start(out=dq_raw[:], in_=dquery.rearrange("(p t) q -> p t q", t=PACK))
+        th_col = col("th_col")
+        nc.gpsimd.dma_start(out=th_col[:], in_=th)
+        load_scale_rows(nc.gpsimd, val_scale_pool, vals_scales, VALS_PLANE)
+
+        key_plane = sb.tile([P, SLOTS], U8, name="key_plane", align_bytes=64)
+        nc.vector.tensor_copy(key_plane[:], key_scale_pool[:].indirect(offsets[:]))
+        val_word_pool = sb.tile([P, TOKENS], U32, name="val_word_pool", tag="key_scales_then_value_words")
+        nc.sync.dma_start(out=val_word_pool[:].bitcast(I32), in_=words_view(vals_words))
+        key_words = sb.tile([P, SLOTS], U32, name="key_words", align_bytes=64)
+        nc.vector.tensor_copy(key_words[:], key_word_pool[:].indirect(offsets[:]))
+        base_sb = sb.tile([P, TOKENS], F32, name="base_sb", tag="key_words_then_base")
+        nc.sync.dma_start(out=base_sb[:], in_=base)
+
+        th2 = affine("th2", th_col, 2.0)
+        q_bf = interleave("q", q_raw)
+        g_raw = sb.tile([P, PACK, ROWS], F32, name="g_raw", tag="query_then_gout")
+        nc.scalar.dma_start(out=g_raw[:], in_=gout.rearrange("(p t) q -> p t q", t=PACK))
+        dq_bf = interleave("dq", dq_raw)
+        a_ps = product("a_ps", quantise("q", q_bf), key_words, key_plane[:])
+        ta_ps = product("ta_ps", quantise("dq", dq_bf), key_words, key_plane[:])
+
+        sq, half_msq4 = wide("sq"), col("half_msq4")
+        nc.scalar.activation(out=sq[:], in_=a_ps[:], func=ACT.Square, scale=1.0 / 16.0, accum_out=half_msq4[:])
+        neg_a, neg_max = wide("neg_a"), col("neg_max")
+        nc.vector.tensor_scalar(out=neg_a[:], in0=a_ps[:], scalar1=-1.0, scalar2=None, op0=ALU.mult, op1=ALU.min,
+                                accum_out=neg_max[:])
+        val_plane = sb.tile([P, SLOTS], U8, name="val_plane", tag="dq_bf16", align_bytes=64)
+        nc.vector.tensor_copy(val_plane[:], val_scale_pool[:].indirect(offsets[:]))
+        g_bf = interleave("g", g_raw)
+        p, z = wide("p"), col("z")
+        nc.scalar.activation(out=p[:], in_=neg_a[:], func=ACT.Exp, scale=-1.0, bias=neg_max[:], accum_out=z[:])
+        t = col("t")
+        nc.scalar.activation(out=t[:], in_=half_msq4[:], func=ACT.Tanh, scale=-1.0, bias=th2[:])
+        c_factor = affine("c_factor", t, 256.0, -256.0)
+        e64 = affine("e64", t, 1.0 / 128.0, 1.0 / 128.0)
+        e64_mean = affine("e64_mean", t, 1.0 / 65536.0, 1.0 / 65536.0)
+        t64 = affine("t64", t, 1.0 / 64.0)
+
+        g_q = quantise("g", g_bf)
+        val_words = sb.tile([P, SLOTS], U32, name="val_words", align_bytes=64)
+        nc.vector.tensor_copy(val_words[:], val_word_pool[:].indirect(offsets[:]))
+        c_ps = product("c_ps", g_q, val_words, val_plane[VALS_PLANE:P, :])
+
+        rz = col("rz")
+        nc.vector.reciprocal(out=rz[:], in_=z[:])
+        w = wide("w")
+        nc.scalar.activation(out=w[:], in_=p[:], func=ACT.Copy, scale=rz[:])
+        prod_a, neg_s = wide("prod_a"), col("neg_s")
+        nc.vector.scalar_tensor_tensor(out=prod_a[:], in0=ta_ps[:], scalar=1.0, in1=neg_a[:], op0=ALU.mult,
+                                       op1=ALU.mult, accum_out=neg_s[:])
+        prod_p, ta_mean = wide("prod_p"), col("ta_mean")
+        nc.vector.scalar_tensor_tensor(out=prod_p[:], in0=ta_ps[:], scalar=rz[:], in1=p[:], op0=ALU.mult,
+                                       op1=ALU.mult, accum_out=ta_mean[:])
+        cs, cs_sum = wide("cs"), col("cs_sum")
+        nc.scalar.activation(out=cs[:], in_=c_ps[:], func=ACT.Copy, scale=c_factor[:], accum_out=cs_sum[:])
+        t0 = affine("t0", neg_s, e64[:], ta_mean[:])
+        b_even = affine("b_even", cs_sum, e64_mean[:])
+        rho = affine("rho", neg_s, t64[:])
+
+        prod_c, neg_cs_mean = wide("prod_c"), col("neg_cs_mean")
+        nc.vector.scalar_tensor_tensor(out=prod_c[:], in0=cs[:], scalar=-1.0, in1=w[:], op0=ALU.mult,
+                                       op1=ALU.mult, accum_out=neg_cs_mean[:])
+        u = wide("u")
+        nc.vector.scalar_tensor_tensor(out=u[:], in0=ta_ps[:], scalar=t0[:], in1=w[:], op0=ALU.subtract,
+                                       op1=ALU.mult)
+        b = affine("b", neg_cs_mean, e64[:], b_even[:])
+        neg_a0 = affine("neg_a0", b, rho[:])
+        ta_term = wide("ta_term")
+        nc.scalar.activation(out=ta_term[:], in_=ta_ps[:], func=ACT.Copy, scale=b[:])
+        neg_x, neg_r = wide("neg_x"), col("neg_r")
+        nc.vector.scalar_tensor_tensor(out=neg_x[:], in0=cs[:], scalar=neg_cs_mean[:], in1=u[:], op0=ALU.add,
+                                       op1=ALU.mult, accum_out=neg_r[:])
+        neg_a_coef = affine("neg_a_coef", neg_r, e64[:], neg_a0[:])
+        soft = wide("soft")
+        nc.vector.scalar_tensor_tensor(out=soft[:], in0=w[:], scalar=neg_r[:], in1=neg_x[:], op0=ALU.mult,
+                                       op1=ALU.subtract)
+        gate = wide("gate")
+        nc.vector.scalar_tensor_tensor(out=gate[:], in0=neg_a[:], scalar=neg_a_coef[:], in1=ta_term[:], op0=ALU.mult,
+                                       op1=ALU.add)
+        nc.vector.tensor_tensor(placed[:].indirect(offsets[:]), soft[:], gate[:], ALU.add)
+
+        for j in range(TOKENS // OUT_CHUNK):
+            cols = slice(j * OUT_CHUNK, (j + 1) * OUT_CHUNK)
+            nc.vector.tensor_tensor(out=base_sb[:, cols], in0=placed[:, cols], in1=base_sb[:, cols], op=ALU.add)
+            nc.sync.dma_start(out=out[:, cols], in_=base_sb[:, cols])

@@ -31,25 +31,29 @@ def tile_attend_hvevenbyspread_s_kernel(tc, query, keys_words, keys_scales, th, 
         sb = ctx.enter_context(tc.tile_pool(name="sb", bufs=1))
         ps = ctx.enter_context(tc.psum_pool(name="ps", bufs=1))
 
-        def col(name):
-            return sb.tile([P, 1], F32, name=name)
+        def col(name, tag=""):
+            return sb.tile([P, 1], F32, name=name, tag=tag or name)
 
-        def wide(name):
-            return sb.tile([P, SLOTS], F32, name=name)
+        def wide(name, tag="", align=None):
+            return sb.tile([P, SLOTS], F32, name=name, tag=tag or name, align_bytes=align)
 
         def words_view(words):
             return words[0].rearrange("p n t -> p (n t)").bitcast(I32)
 
-        def load_scale_rows(queue, window, scales, first):
-            for quad in range(4):
+        def load_scale_rows(queues, window, scales, first):
+            for quad, queue in enumerate(queues):
                 row = 32 * quad + first
                 queue.dma_start(out=window[row:row + 4, :].bitcast(I32),
                                 in_=scales[0, 4 * quad:4 * quad + 4, :].bitcast(I32))
 
-        def interleave(name, raw):
+        def interleave(name, raw, on_vector=False):
             grouped = sb.tile([P, ROWS * PACK], BF16, name=name + "_bf16", tag=name + "_bf16", align_bytes=64)
-            nc.scalar.activation(out=grouped[:].rearrange("p (c i t) -> p c t i", i=4, t=PACK),
-                                 in_=raw[:].rearrange("p t (c i) -> p c t i", i=4), func=ACT.Copy)
+            dst = grouped[:].rearrange("p (c i t) -> p c t i", i=4, t=PACK)
+            src = raw[:].rearrange("p t (c i) -> p c t i", i=4)
+            if on_vector:
+                nc.vector.tensor_copy(out=dst, in_=src)
+            else:
+                nc.scalar.activation(out=dst, in_=src, func=ACT.Copy)
             return grouped
 
         def quantise(name, grouped):
@@ -71,73 +75,74 @@ def tile_attend_hvevenbyspread_s_kernel(tc, query, keys_words, keys_scales, th, 
 
         offsets = sb.tile([P, SLOTS // 16], U16, name="offsets")
         nc.sync.dma_start(offsets[:], offs)
-        key_scale_pool = sb.tile([P, TOKENS], U8, name="key_scale_pool", tag="key_scales_then_value_words")
-        val_scale_pool = sb.tile([P, TOKENS], U8, name="val_scale_pool")
+        key_scale_pool = sb.tile([P, TOKENS], U8, name="key_scale_pool")
+        val_scale_pool = sb.tile([P, TOKENS], U8, name="val_scale_pool", tag="value_scales_then_scores")
         nc.vector.memset(key_scale_pool[:].bitcast(I32), 0)
         nc.vector.memset(val_scale_pool[:].bitcast(I32), 0)
         placed = sb.tile([P, TOKENS], F32, name="placed")
         nc.vector.memset(placed[:], 0.0)
 
-        key_word_pool = sb.tile([P, TOKENS], U32, name="key_word_pool", tag="key_words_then_base")
-        nc.sync.dma_start(out=key_word_pool[:].bitcast(I32), in_=words_view(keys_words))
-        load_scale_rows(nc.scalar, key_scale_pool, keys_scales, 0)
-        q_raw = sb.tile([P, PACK, ROWS], F32, name="q_raw", tag="query_then_gout")
+        q_raw = sb.tile([P, PACK, ROWS], F32, name="q_raw", tag="query_then_th")
         nc.sync.dma_start(out=q_raw[:], in_=query.rearrange("(p t) q -> p t q", t=PACK))
-        dq_raw = sb.tile([P, PACK, ROWS], F32, name="dq_raw")
+        key_word_pool = sb.tile([P, TOKENS], U32, name="key_word_pool")
+        nc.sync.dma_start(out=key_word_pool[:].bitcast(I32), in_=words_view(keys_words))
+        load_scale_rows([nc.scalar] * 4, key_scale_pool, keys_scales, 0)
+        dq_raw = sb.tile([P, PACK, ROWS], F32, name="dq_raw", tag="dquery_then_gout")
         nc.sync.dma_start(out=dq_raw[:], in_=dquery.rearrange("(p t) q -> p t q", t=PACK))
-        th_col = col("th_col")
-        nc.gpsimd.dma_start(out=th_col[:], in_=th)
-        load_scale_rows(nc.gpsimd, val_scale_pool, vals_scales, VALS_PLANE)
+        val_word_pool = sb.tile([P, TOKENS], U32, name="val_word_pool", tag="value_words_then_base")
+        nc.sync.dma_start(out=val_word_pool[:].bitcast(I32), in_=words_view(vals_words))
+        load_scale_rows([nc.scalar, nc.scalar, nc.gpsimd, nc.gpsimd], val_scale_pool, vals_scales, VALS_PLANE)
+
 
         key_plane = sb.tile([P, SLOTS], U8, name="key_plane", align_bytes=64)
         nc.vector.tensor_copy(key_plane[:], key_scale_pool[:].indirect(offsets[:]))
-        val_word_pool = sb.tile([P, TOKENS], U32, name="val_word_pool", tag="key_scales_then_value_words")
-        nc.sync.dma_start(out=val_word_pool[:].bitcast(I32), in_=words_view(vals_words))
+        q_q = quantise("q", interleave("q", q_raw, on_vector=True))
+        th_col = col("th_col", "query_then_th")
+        nc.gpsimd.dma_start(out=th_col[:], in_=th)
         key_words = sb.tile([P, SLOTS], U32, name="key_words", align_bytes=64)
         nc.vector.tensor_copy(key_words[:], key_word_pool[:].indirect(offsets[:]))
-        base_sb = sb.tile([P, TOKENS], F32, name="base_sb", tag="key_words_then_base")
-        nc.sync.dma_start(out=base_sb[:], in_=base)
-
-        th2 = affine("th2", th_col, 2.0)
-        q_bf = interleave("q", q_raw)
-        g_raw = sb.tile([P, PACK, ROWS], F32, name="g_raw", tag="query_then_gout")
-        nc.scalar.dma_start(out=g_raw[:], in_=gout.rearrange("(p t) q -> p t q", t=PACK))
         dq_bf = interleave("dq", dq_raw)
-        a_ps = product("a_ps", quantise("q", q_bf), key_words, key_plane[:])
+        g_raw = sb.tile([P, PACK, ROWS], F32, name="g_raw", tag="dquery_then_gout")
+        nc.scalar.dma_start(out=g_raw[:], in_=gout.rearrange("(p t) q -> p t q", t=PACK))
+        a_ps = product("a_ps", q_q, key_words, key_plane[:])
         ta_ps = product("ta_ps", quantise("dq", dq_bf), key_words, key_plane[:])
 
-        sq, half_msq4 = wide("sq"), col("half_msq4")
-        nc.scalar.activation(out=sq[:], in_=a_ps[:], func=ACT.Square, scale=1.0 / 16.0, accum_out=half_msq4[:])
-        neg_a, neg_max = wide("neg_a"), col("neg_max")
-        nc.vector.tensor_scalar(out=neg_a[:], in0=a_ps[:], scalar1=-1.0, scalar2=None, op0=ALU.mult, op1=ALU.min,
-                                accum_out=neg_max[:])
         val_plane = sb.tile([P, SLOTS], U8, name="val_plane", tag="dq_bf16", align_bytes=64)
         nc.vector.tensor_copy(val_plane[:], val_scale_pool[:].indirect(offsets[:]))
-        g_bf = interleave("g", g_raw)
-        p, z = wide("p"), col("z")
-        nc.scalar.activation(out=p[:], in_=neg_a[:], func=ACT.Exp, scale=-1.0, bias=neg_max[:], accum_out=z[:])
+
+        th2 = affine("th2", th_col, 2.0)
+        sq, half_msq4 = wide("sq"), col("half_msq4")
+        nc.scalar.activation(out=sq[:], in_=a_ps[:], func=ACT.Square, scale=1.0 / 16.0, accum_out=half_msq4[:])
         t = col("t")
         nc.scalar.activation(out=t[:], in_=half_msq4[:], func=ACT.Tanh, scale=-1.0, bias=th2[:])
         c_factor = affine("c_factor", t, 256.0, -256.0)
         e64 = affine("e64", t, 1.0 / 128.0, 1.0 / 128.0)
         e64_mean = affine("e64_mean", t, 1.0 / 65536.0, 1.0 / 65536.0)
         t64 = affine("t64", t, 1.0 / 64.0)
+        neg_a, neg_max = wide("neg_a", "value_scales_then_scores"), col("neg_max")
+        nc.vector.tensor_scalar(out=neg_a[:], in0=a_ps[:], scalar1=-1.0, scalar2=None, op0=ALU.mult, op1=ALU.min,
+                                accum_out=neg_max[:])
+        p, z = wide("p"), col("z")
+        nc.scalar.activation(out=p[:], in_=neg_a[:], func=ACT.Exp, scale=-1.0, bias=neg_max[:], accum_out=z[:])
+        g_bf = interleave("g", g_raw)
 
         g_q = quantise("g", g_bf)
         val_words = sb.tile([P, SLOTS], U32, name="val_words", align_bytes=64)
         nc.vector.tensor_copy(val_words[:], val_word_pool[:].indirect(offsets[:]))
         c_ps = product("c_ps", g_q, val_words, val_plane[VALS_PLANE:P, :])
 
-        rz = col("rz")
+        rz = col("rz", "value_words_then_base")
         nc.vector.reciprocal(out=rz[:], in_=z[:])
-        w = wide("w")
+        w = wide("w", "dquery_then_gout")
         nc.scalar.activation(out=w[:], in_=p[:], func=ACT.Copy, scale=rz[:])
-        prod_a, neg_s = wide("prod_a"), col("neg_s")
+        prod_a, neg_s = wide("prod_a", "g_bf16", 64), col("neg_s")
         nc.vector.scalar_tensor_tensor(out=prod_a[:], in0=ta_ps[:], scalar=1.0, in1=neg_a[:], op0=ALU.mult,
                                        op1=ALU.mult, accum_out=neg_s[:])
-        prod_p, ta_mean = wide("prod_p"), col("ta_mean")
+        prod_p, ta_mean = wide("prod_p", "g_bf16", 64), col("ta_mean")
         nc.vector.scalar_tensor_tensor(out=prod_p[:], in0=ta_ps[:], scalar=rz[:], in1=p[:], op0=ALU.mult,
                                        op1=ALU.mult, accum_out=ta_mean[:])
+        base_sb = sb.tile([P, TOKENS], F32, name="base_sb", tag="value_words_then_base")
+        nc.sync.dma_start(out=base_sb[:], in_=base)
         cs, cs_sum = wide("cs"), col("cs_sum")
         nc.scalar.activation(out=cs[:], in_=c_ps[:], func=ACT.Copy, scale=c_factor[:], accum_out=cs_sum[:])
         t0 = affine("t0", neg_s, e64[:], ta_mean[:])

@@ -82,35 +82,36 @@ def tile_attend_hvevenbyspread_s_kernel(tc, query, keys_words, keys_scales, th, 
         placed = sb.tile([P, TOKENS], F32, name="placed")
         nc.vector.memset(placed[:], 0.0)
 
-        q_raw = sb.tile([P, PACK, ROWS], F32, name="q_raw", tag="query_then_th")
+        q_raw = sb.tile([P, PACK, ROWS], F32, name="q_raw", tag="query_then_gout")
         nc.sync.dma_start(out=q_raw[:], in_=query.rearrange("(p t) q -> p t q", t=PACK))
-        key_word_pool = sb.tile([P, TOKENS], U32, name="key_word_pool")
-        nc.sync.dma_start(out=key_word_pool[:].bitcast(I32), in_=words_view(keys_words))
-        load_scale_rows([nc.scalar] * 4, key_scale_pool, keys_scales, 0)
-        dq_raw = sb.tile([P, PACK, ROWS], F32, name="dq_raw", tag="dquery_then_gout")
+        dq_raw = sb.tile([P, PACK, ROWS], F32, name="dq_raw", tag="dquery_then_value_words")
         nc.sync.dma_start(out=dq_raw[:], in_=dquery.rearrange("(p t) q -> p t q", t=PACK))
-        val_word_pool = sb.tile([P, TOKENS], U32, name="val_word_pool", tag="value_words_then_base")
+        key_word_pool = sb.tile([P, TOKENS], U32, name="key_word_pool", tag="key_words_then_value_plane",
+                                align_bytes=64)
+        nc.sync.dma_start(out=key_word_pool[:].bitcast(I32), in_=words_view(keys_words))
+        th_col = col("th_col")
+        nc.gpsimd.dma_start(out=th_col[:], in_=th)
+        load_scale_rows([nc.scalar] * 4, key_scale_pool, keys_scales, 0)
+        load_scale_rows([nc.scalar] * 3 + [nc.gpsimd], val_scale_pool, vals_scales, VALS_PLANE)
+
+        q_bf = interleave("q", q_raw, on_vector=True)
+        g_raw = sb.tile([P, PACK, ROWS], F32, name="g_raw", tag="query_then_gout")
+        dq_bf = interleave("dq", dq_raw, on_vector=True)
+        val_word_pool = sb.tile([P, TOKENS], U32, name="val_word_pool", tag="dquery_then_value_words")
         nc.sync.dma_start(out=val_word_pool[:].bitcast(I32), in_=words_view(vals_words))
-        load_scale_rows([nc.scalar, nc.scalar, nc.gpsimd, nc.gpsimd], val_scale_pool, vals_scales, VALS_PLANE)
-
-
+        q_q = quantise("q", q_bf)
+        dq_q = quantise("dq", dq_bf)
         key_plane = sb.tile([P, SLOTS], U8, name="key_plane", align_bytes=64)
         nc.vector.tensor_copy(key_plane[:], key_scale_pool[:].indirect(offsets[:]))
-        q_q = quantise("q", interleave("q", q_raw, on_vector=True))
-        th_col = col("th_col", "query_then_th")
-        nc.gpsimd.dma_start(out=th_col[:], in_=th)
+        th2 = affine("th2", th_col, 2.0)
+        nc.scalar.dma_start(out=g_raw[:], in_=gout.rearrange("(p t) q -> p t q", t=PACK))
         key_words = sb.tile([P, SLOTS], U32, name="key_words", align_bytes=64)
         nc.vector.tensor_copy(key_words[:], key_word_pool[:].indirect(offsets[:]))
-        dq_bf = interleave("dq", dq_raw)
-        g_raw = sb.tile([P, PACK, ROWS], F32, name="g_raw", tag="dquery_then_gout")
-        nc.scalar.dma_start(out=g_raw[:], in_=gout.rearrange("(p t) q -> p t q", t=PACK))
         a_ps = product("a_ps", q_q, key_words, key_plane[:])
-        ta_ps = product("ta_ps", quantise("dq", dq_bf), key_words, key_plane[:])
-
-        val_plane = sb.tile([P, SLOTS], U8, name="val_plane", tag="dq_bf16", align_bytes=64)
+        ta_ps = product("ta_ps", dq_q, key_words, key_plane[:])
+        val_plane = sb.tile([P, SLOTS], U8, name="val_plane", tag="key_words_then_value_plane", align_bytes=64)
         nc.vector.tensor_copy(val_plane[:], val_scale_pool[:].indirect(offsets[:]))
 
-        th2 = affine("th2", th_col, 2.0)
         sq, half_msq4 = wide("sq"), col("half_msq4")
         nc.scalar.activation(out=sq[:], in_=a_ps[:], func=ACT.Square, scale=1.0 / 16.0, accum_out=half_msq4[:])
         t = col("t")
@@ -122,18 +123,18 @@ def tile_attend_hvevenbyspread_s_kernel(tc, query, keys_words, keys_scales, th, 
         neg_a, neg_max = wide("neg_a", "value_scales_then_scores"), col("neg_max")
         nc.vector.tensor_scalar(out=neg_a[:], in0=a_ps[:], scalar1=-1.0, scalar2=None, op0=ALU.mult, op1=ALU.min,
                                 accum_out=neg_max[:])
-        p, z = wide("p"), col("z")
-        nc.scalar.activation(out=p[:], in_=neg_a[:], func=ACT.Exp, scale=-1.0, bias=neg_max[:], accum_out=z[:])
         g_bf = interleave("g", g_raw)
+        p, z = wide("p", "query_then_gout"), col("z")
+        nc.scalar.activation(out=p[:], in_=neg_a[:], func=ACT.Exp, scale=-1.0, bias=neg_max[:], accum_out=z[:])
 
         g_q = quantise("g", g_bf)
         val_words = sb.tile([P, SLOTS], U32, name="val_words", align_bytes=64)
         nc.vector.tensor_copy(val_words[:], val_word_pool[:].indirect(offsets[:]))
         c_ps = product("c_ps", g_q, val_words, val_plane[VALS_PLANE:P, :])
 
-        rz = col("rz", "value_words_then_base")
+        rz = col("rz", "dquery_then_value_words")
         nc.vector.reciprocal(out=rz[:], in_=z[:])
-        w = wide("w", "dquery_then_gout")
+        w = wide("w")
         nc.scalar.activation(out=w[:], in_=p[:], func=ACT.Copy, scale=rz[:])
         prod_a, neg_s = wide("prod_a", "g_bf16", 64), col("neg_s")
         nc.vector.scalar_tensor_tensor(out=prod_a[:], in0=ta_ps[:], scalar=1.0, in1=neg_a[:], op0=ALU.mult,
@@ -141,7 +142,7 @@ def tile_attend_hvevenbyspread_s_kernel(tc, query, keys_words, keys_scales, th, 
         prod_p, ta_mean = wide("prod_p", "g_bf16", 64), col("ta_mean")
         nc.vector.scalar_tensor_tensor(out=prod_p[:], in0=ta_ps[:], scalar=rz[:], in1=p[:], op0=ALU.mult,
                                        op1=ALU.mult, accum_out=ta_mean[:])
-        base_sb = sb.tile([P, TOKENS], F32, name="base_sb", tag="value_words_then_base")
+        base_sb = sb.tile([P, TOKENS], F32, name="base_sb", tag="dquery_then_value_words")
         nc.sync.dma_start(out=base_sb[:], in_=base)
         cs, cs_sum = wide("cs"), col("cs_sum")
         nc.scalar.activation(out=cs[:], in_=c_ps[:], func=ACT.Copy, scale=c_factor[:], accum_out=cs_sum[:])

from contextlib import ExitStack

import concourse.mybir as mybir

F32 = mybir.dt.float32
BF16 = mybir.dt.bfloat16
I32 = mybir.dt.int32
U32 = mybir.dt.uint32
U16 = mybir.dt.uint16
U8 = mybir.dt.uint8
FP8X4 = mybir.dt.float8_e4m3fn_x4
ALU = mybir.AluOpType
ACT = mybir.ActivationFunctionType

P = 128
PACK = 4
TOKENS = 2048
SLOTS = 512
ROWS = 128
FEATURES = 512
VALS_PLANE = 4
OUT_CHUNK = 512

FLOPS = 3 * 2 * FEATURES * ROWS * SLOTS


def tile_attend_hvevenbyspread_s_kernel(tc, query, keys_words, keys_scales, th, gout, vals_words, vals_scales,
                                         dquery, base, offs, out):
    nc = tc.nc
    with ExitStack() as ctx:
        sb = ctx.enter_context(tc.tile_pool(name="sb", bufs=1))
        ps = ctx.enter_context(tc.psum_pool(name="ps", bufs=1))

        def col(name, tag=""):
            return sb.tile([P, 1], F32, name=name, tag=tag or name)

        def wide(name, tag="", align=None):
            return sb.tile([P, SLOTS], F32, name=name, tag=tag or name, align_bytes=align)

        def words_view(words):
            return words[0].rearrange("p n t -> p (n t)").bitcast(I32)

        def load_scale_rows(queues, window, scales, first):
            for quad, queue in enumerate(queues):
                row = 32 * quad + first
                queue.dma_start(out=window[row:row + 4, :].bitcast(I32),
                                in_=scales[0, 4 * quad:4 * quad + 4, :].bitcast(I32))

        def interleave(name, raw, on_vector=False):
            grouped = sb.tile([P, ROWS * PACK], BF16, name=name + "_bf16", tag=name + "_bf16", align_bytes=64)
            dst = grouped[:].rearrange("p (c i t) -> p c t i", i=4, t=PACK)
            src = raw[:].rearrange("p t (c i) -> p c t i", i=4)
            if on_vector:
                nc.vector.tensor_copy(out=dst, in_=src)
            else:
                nc.scalar.activation(out=dst, in_=src, func=ACT.Copy)
            return grouped

        def quantise(name, grouped):
            codes = sb.tile([P, ROWS], U32, name=name + "_codes", align_bytes=64)
            plane = sb.tile([P, ROWS], U8, name=name + "_plane", align_bytes=64)
            nc.vector.quantize_mx(out=codes[:].bitcast(FP8X4), scales=plane[:], in_=grouped[:])
            return codes, plane

        def product(name, rows_q, words, plane):
            acc = ps.tile([ROWS, SLOTS], F32, name=name)
            nc.tensor.matmul_mx(out=acc[:], lhsT=rows_q[0][:].bitcast(FP8X4), lhsT_scale=rows_q[1][:],
                                rhs=words[:].bitcast(FP8X4), rhs_scale=plane, start=True, stop=True)
            return acc

        def affine(name, x, scale, bias=0.0):
            y = col(name)
            nc.scalar.activation(out=y[:], in_=x[:], func=ACT.Identity, scale=scale, bias=bias)
            return y

        offsets = sb.tile([P, SLOTS // 16], U16, name="offsets")
        nc.sync.dma_start(offsets[:], offs)
        key_scale_pool = sb.tile([P, TOKENS], U8, name="key_scale_pool")
        val_scale_pool = sb.tile([P, TOKENS], U8, name="val_scale_pool", tag="value_scales_then_scores")
        nc.vector.memset(key_scale_pool[:].bitcast(I32), 0)
        nc.vector.memset(val_scale_pool[:].bitcast(I32), 0)
        placed = sb.tile([P, TOKENS], F32, name="placed")
        nc.vector.memset(placed[:], 0.0)

        q_raw = sb.tile([P, PACK, ROWS], F32, name="q_raw", tag="query_then_gout")
        nc.sync.dma_start(out=q_raw[:], in_=query.rearrange("(p t) q -> p t q", t=PACK))
        dq_raw = sb.tile([P, PACK, ROWS], F32, name="dq_raw", tag="dquery_then_value_words")
        nc.sync.dma_start(out=dq_raw[:], in_=dquery.rearrange("(p t) q -> p t q", t=PACK))
        key_word_pool = sb.tile([P, TOKENS], U32, name="key_word_pool", tag="key_words_then_value_plane",
                                align_bytes=64)
        nc.sync.dma_start(out=key_word_pool[:].bitcast(I32), in_=words_view(keys_words))
        th_col = col("th_col")
        nc.gpsimd.dma_start(out=th_col[:], in_=th)
        load_scale_rows([nc.scalar] * 4, key_scale_pool, keys_scales, 0)
        load_scale_rows([nc.scalar] * 3 + [nc.gpsimd], val_scale_pool, vals_scales, VALS_PLANE)

        q_bf = interleave("q", q_raw, on_vector=True)
        g_raw = sb.tile([P, PACK, ROWS], F32, name="g_raw", tag="query_then_gout")
        dq_bf = interleave("dq", dq_raw, on_vector=True)
        val_word_pool = sb.tile([P, TOKENS], U32, name="val_word_pool", tag="dquery_then_value_words")
        nc.sync.dma_start(out=val_word_pool[:].bitcast(I32), in_=words_view(vals_words))
        q_q = quantise("q", q_bf)
        dq_q = quantise("dq", dq_bf)
        key_plane = sb.tile([P, SLOTS], U8, name="key_plane", align_bytes=64)
        nc.vector.tensor_copy(key_plane[:], key_scale_pool[:].indirect(offsets[:]))
        th2 = affine("th2", th_col, 2.0)
        nc.scalar.dma_start(out=g_raw[:], in_=gout.rearrange("(p t) q -> p t q", t=PACK))
        key_words = sb.tile([P, SLOTS], U32, name="key_words", align_bytes=64)
        nc.vector.tensor_copy(key_words[:], key_word_pool[:].indirect(offsets[:]))
        a_ps = product("a_ps", q_q, key_words, key_plane[:])
        ta_ps = product("ta_ps", dq_q, key_words, key_plane[:])
        val_plane = sb.tile([P, SLOTS], U8, name="val_plane", tag="key_words_then_value_plane", align_bytes=64)
        nc.vector.tensor_copy(val_plane[:], val_scale_pool[:].indirect(offsets[:]))

        sq, half_msq4 = wide("sq"), col("half_msq4")
        nc.scalar.activation(out=sq[:], in_=a_ps[:], func=ACT.Square, scale=1.0 / 16.0, accum_out=half_msq4[:])
        t = col("t")
        nc.scalar.activation(out=t[:], in_=half_msq4[:], func=ACT.Tanh, scale=-1.0, bias=th2[:])
        c_factor = affine("c_factor", t, 256.0, -256.0)
        e64 = affine("e64", t, 1.0 / 128.0, 1.0 / 128.0)
        e64_mean = affine("e64_mean", t, 1.0 / 65536.0, 1.0 / 65536.0)
        t64 = affine("t64", t, 1.0 / 64.0)
        neg_a, neg_max = wide("neg_a", "value_scales_then_scores"), col("neg_max")
        nc.vector.tensor_scalar(out=neg_a[:], in0=a_ps[:], scalar1=-1.0, scalar2=None, op0=ALU.mult, op1=ALU.min,
                                accum_out=neg_max[:])
        g_bf = interleave("g", g_raw)
        p, z = wide("p", "query_then_gout"), col("z")
        nc.scalar.activation(out=p[:], in_=neg_a[:], func=ACT.Exp, scale=-1.0, bias=neg_max[:], accum_out=z[:])

        g_q = quantise("g", g_bf)
        val_words = sb.tile([P, SLOTS], U32, name="val_words", align_bytes=64)
        nc.vector.tensor_copy(val_words[:], val_word_pool[:].indirect(offsets[:]))
        c_ps = product("c_ps", g_q, val_words, val_plane[VALS_PLANE:P, :])

        rz = col("rz", "dquery_then_value_words")
        nc.vector.reciprocal(out=rz[:], in_=z[:])
        w = wide("w")
        nc.scalar.activation(out=w[:], in_=p[:], func=ACT.Copy, scale=rz[:])
        prod_a, neg_s = wide("prod_a", "g_bf16", 64), col("neg_s")
        nc.vector.scalar_tensor_tensor(out=prod_a[:], in0=ta_ps[:], scalar=1.0, in1=neg_a[:], op0=ALU.mult,
                                       op1=ALU.mult, accum_out=neg_s[:])
        prod_p, ta_mean = wide("prod_p", "g_bf16", 64), col("ta_mean")
        nc.vector.scalar_tensor_tensor(out=prod_p[:], in0=ta_ps[:], scalar=rz[:], in1=p[:], op0=ALU.mult,
                                       op1=ALU.mult, accum_out=ta_mean[:])
        base_sb = sb.tile([P, TOKENS], F32, name="base_sb", tag="dquery_then_value_words")
        nc.sync.dma_start(out=base_sb[:], in_=base)
        cs, cs_sum = wide("cs"), col("cs_sum")
        nc.scalar.activation(out=cs[:], in_=c_ps[:], func=ACT.Copy, scale=c_factor[:], accum_out=cs_sum[:])
        t0 = affine("t0", neg_s, e64[:], ta_mean[:])
        b_even = affine("b_even", cs_sum, e64_mean[:])
        rho = affine("rho", neg_s, t64[:])

        prod_c, neg_cs_mean = wide("prod_c"), col("neg_cs_mean")
        nc.vector.scalar_tensor_tensor(out=prod_c[:], in0=cs[:], scalar=-1.0, in1=w[:], op0=ALU.mult,
                                       op1=ALU.mult, accum_out=neg_cs_mean[:])
        u = wide("u")
        nc.vector.scalar_tensor_tensor(out=u[:], in0=ta_ps[:], scalar=t0[:], in1=w[:], op0=ALU.subtract,
                                       op1=ALU.mult)
        b = affine("b", neg_cs_mean, e64[:], b_even[:])
        neg_a0 = affine("neg_a0", b, rho[:])
        ta_term = wide("ta_term")
        nc.scalar.activation(out=ta_term[:], in_=ta_ps[:], func=ACT.Copy, scale=b[:])
        neg_x, neg_r = wide("neg_x"), col("neg_r")
        nc.vector.scalar_tensor_tensor(out=neg_x[:], in0=cs[:], scalar=neg_cs_mean[:], in1=u[:], op0=ALU.add,
                                       op1=ALU.mult, accum_out=neg_r[:])
        neg_a_coef = affine("neg_a_coef", neg_r, e64[:], neg_a0[:])
        soft = wide("soft")
        nc.vector.scalar_tensor_tensor(out=soft[:], in0=w[:], scalar=neg_r[:], in1=neg_x[:], op0=ALU.mult,
                                       op1=ALU.subtract)
        gate = wide("gate")
        nc.vector.scalar_tensor_tensor(out=gate[:], in0=neg_a[:], scalar=neg_a_coef[:], in1=ta_term[:], op0=ALU.mult,
                                       op1=ALU.add)
        nc.vector.tensor_tensor(placed[:].indirect(offsets[:]), soft[:], gate[:], ALU.add)

        for j in range(TOKENS // OUT_CHUNK):
            cols = slice(j * OUT_CHUNK, (j + 1) * OUT_CHUNK)
            nc.vector.tensor_tensor(out=base_sb[:, cols], in0=placed[:, cols], in1=base_sb[:, cols], op=ALU.add)
            nc.sync.dma_start(out=out[:, cols], in_=base_sb[:, cols])
